import numpy as np
CORES = [56,57,58,59,60,61,62,63,440,441,442,443,444,445,446,447]
N = 16
ROOT = 12
def setup_inputs(rng):
    return {"x": rng.standard_normal((N, 128, 64), dtype=np.float32)}
def reference(x):
    y = np.full((N, 128, N * 64), np.nan, x.dtype)
    y[ROOT] = np.concatenate(list(x), axis=1)
    return {"y": y}

W = 64

SCRATCH = {
    "land": ("sbuf", [128, 16 * W], "float32"),
}
SEMAPHORES = ["loaded", "sent", "near", "far", "stored"]


def _engines(mask):
    return sum((mask >> k) & 1 for k in range(16))


def rank_program(g, core, T, topo):
    rank = T.rank_of(core)
    if rank is None:
        return

    cores = list(T.cores)
    root_rank = 12 if T.root is None else T.root
    root = cores[root_rank]
    on_chip = lambda c: (topo.host(c), topo.chip(c)) == (topo.host(root), topo.chip(root))
    slot = T.land[:, rank * W:(rank + 1) * W]

    if core != root:
        g.sync.dma_start(slot, T.x[:]).then_inc(T.sem.loaded, 16)
        g.wait_ge(T.sem.loaded, 16)
        rid, pid = topo.addr(root, core)
        mask = topo.mask(core, root)
        g.remote_dma(slot, slot, T.sem.near if on_chip(core) else T.sem.far, T.sem.sent, pid, rid, mask)
        g.wait_ge(T.sem.sent, _engines(mask))
        return

    near_total = 16 + sum(_engines(topo.mask(c, root)) for c in cores if c != root and on_chip(c))
    far_total = sum(_engines(topo.mask(c, root)) for c in cores if not on_chip(c))
    half = 8 * W

    g.sync.dma_start(slot, T.x[:]).then_inc(T.sem.near, 16)
    g.sync.wait_ge(T.sem.near, near_total)
    g.sync.dma_start(T.y[:, half:2 * half], T.land[:, half:2 * half]).then_inc(T.sem.stored, 16)

    g.scalar.wait_ge(T.sem.far, far_total)
    g.scalar.dma_start(T.y[:, 0:half], T.land[:, 0:half]).then_inc(T.sem.stored, 16)

    g.wait_ge(T.sem.stored, 32)
